import numpy as np
import ml_dtypes


def mxq(x, axis, fmt="e4m3"):
    dtype, down = {"e4m3": (ml_dtypes.float8_e4m3fn, 7), "e5m2": (ml_dtypes.float8_e5m2, 14)}[fmt]
    v = np.moveaxis(np.asarray(x, np.float32).astype(ml_dtypes.bfloat16).astype(np.float64), axis, -1)
    blocks = v.reshape(v.shape[:-1] + (-1, 32))
    amax = np.abs(blocks).max(-1, keepdims=True)
    byte = np.maximum(np.where(amax > 0, np.frexp(amax)[1] - 1 + 127, 0) - down, 1)
    scale = np.exp2(byte - 127.0)
    codes = (blocks / scale).astype(np.float32).astype(dtype).astype(np.float64)
    return np.moveaxis((codes * scale).reshape(v.shape), -1, axis)


WIDE = False


def mx_kscale(k):
    if not WIDE:
        return np.ones(k)
    levels = np.array([10, -10, 5, -5, 0])
    if k % 512:
        return np.exp2(np.random.permutation(np.resize(levels, k // 32))).repeat(32)
    a = np.empty((k // 512, 16))
    for p in range(k // 512):
        a[p, :8] = np.random.permutation(np.resize(levels, 8))
        for g in range(8):
            far = levels[np.abs(levels - a[p, g]) >= 10]
            a[p, g + 8] = far[np.random.randint(len(far))]
    return np.exp2(a.ravel()).repeat(32)


def f64(x):
    return np.asarray(x).astype(np.float64)


def striped(idx):
    return np.tile(np.asarray(idx).reshape(-1, 16).T, (8, 1)).astype(np.uint16)


def unstriped(offs):
    return offs[:16].T.reshape(-1).astype(np.int64)


E2M1 = np.array([0.0, 0.5, 1.0, 1.5, 2.0, 3.0, 4.0, 6.0, -0.0, -0.5, -1.0, -1.5, -2.0, -3.0, -4.0, -6.0])


def pack_weight(w, fmt):
    k, n = w.shape
    w = f64(np.asarray(w, np.float32).astype(ml_dtypes.bfloat16)).reshape(k // 32, 32, n)
    amax = np.abs(w).max(1)
    if fmt == "e4m3":
        byte = np.frexp(amax)[1] - 1 + 127 - 7
    else:
        mant, ex = np.frexp(amax / 6.0)
        byte = np.where(mant > 0.5, ex, ex - 1) + 127
    byte = np.clip(np.where(amax > 0, byte, 1), 1, 254)
    scaled = (w * np.exp2(127.0 - byte)[:, None, :]).reshape(k, n).astype(np.float32)
    by_word = np.ascontiguousarray(scaled.reshape(k // 512, 128, 4, n).transpose(0, 1, 3, 2))
    if fmt == "e4m3":
        words = by_word.astype(ml_dtypes.float8_e4m3fn).view(np.uint8)
    else:
        c = by_word.astype(ml_dtypes.float4_e2m1fn).view(np.uint8) & 0xF
        words = (c[..., 0::2] | (c[..., 1::2] << 4)).reshape(k // 512, 128, 2 * n)
    return np.ascontiguousarray(words), np.ascontiguousarray(byte.astype(np.uint8).reshape(k // 512, 16, n))


def unpack_weight(words, scales, fmt):
    g, _, n = scales.shape
    words = np.ascontiguousarray(words).reshape(g, 128, n, -1)
    if fmt == "e4m3":
        vals = words.view(ml_dtypes.float8_e4m3fn).astype(np.float64)
    else:
        nib = np.empty((g, 128, n, 4), np.uint8)
        nib[..., 0::2] = words & 0xF
        nib[..., 1::2] = words >> 4
        vals = E2M1[nib]
    vals = vals * np.repeat(np.exp2(scales.astype(np.float64) - 127.0), 8, axis=1)[..., None]
    return vals.transpose(0, 1, 3, 2).reshape(g * 512, n)


def bf(x):
    return np.asarray(x, np.float32).astype(ml_dtypes.bfloat16)


def planes(Y):
    r, m = Y.shape
    b = f64(bf(Y)).reshape(r // 32, 32, m)
    amax = np.abs(b).max(1)
    byte = np.clip(np.where(amax > 0, np.frexp(amax)[1] - 1 + 127 - 7, 1), 1, 254)
    codes = (b * np.exp2(127.0 - byte)[:, None, :]).reshape(r, m).astype(np.float32).astype(ml_dtypes.float8_e4m3fn).view(np.uint8)
    words = codes.reshape(r // 512, 128, 4, m).transpose(0, 1, 3, 2)
    return np.ascontiguousarray(words), np.ascontiguousarray(byte.astype(np.uint8).reshape(r // 512, 16, m))


K, T, J, R, N = 1024, 1024, 512, 512, 512


def setup_inputs():
    n = np.random.standard_normal
    idx = np.random.permutation(T)[:J]
    fk = mx_kscale(K)
    fr = mx_kscale(R)
    xtp = pack_weight(n((K, T)) / fk[:, None], "e2m1")
    wap = pack_weight(n((K, R)) * 1 / np.sqrt(K) * fk[:, None] * fr, "e4m3")
    wbp = pack_weight(n((R, N)) * 1 / np.sqrt(R) / fr[:, None], "e2m1")
    return {
        "xt_words": xtp[0],
        "xt_scales": xtp[1],
        "wa_words": wap[0],
        "wa_scales": wap[1],
        "old": (n((R, T)) * fr[:, None]).astype(np.float32),
        "wb_words": wbp[0],
        "wb_scales": wbp[1],
        "offs": striped(idx),
    }


def reference(xt_words, xt_scales, wa_words, wa_scales, old, wb_words, wb_scales, offs):
    idx = unstriped(offs)
    xtu = unpack_weight(xt_words, xt_scales, "e2m1")
    wau = unpack_weight(wa_words, wa_scales, "e4m3")
    wbu = unpack_weight(wb_words, wb_scales, "e2m1")
    xtidxg = xtu[:, idx]
    a = wau.T @ xtidxg
    h1 = np.maximum(a, 0.0)
    hp = np.zeros((R, T))
    hp[:, idx] = h1
    pg = hp + 0.5 * f64(old)
    pgq = mxq(pg, 0, "e4m3")
    y = wbu.T @ pgq
    words, scales = planes(y)
    return y, words, scales

@@ -1,0 +1,275 @@
+from contextlib import ExitStack
+
+import concourse.mybir as mybir
+from concourse.masks import make_identity
+
+K, T, J, R, N = 1024, 1024, 512, 512, 512
+FLOPS = 2 * K * R * J + 2 * R * N * T
+
+F32 = mybir.dt.float32
+BF16 = mybir.dt.bfloat16
+I32 = mybir.dt.int32
+U32 = mybir.dt.uint32
+U16 = mybir.dt.uint16
+U8 = mybir.dt.uint8
+FP8X4 = mybir.dt.float8_e4m3fn_x4
+FP4X4 = mybir.dt.float4_e2m1fn_x4
+ACT = mybir.ActivationFunctionType
+ALU = mybir.AluOpType
+
+P = 128
+PACK = 4
+PASSES = K // (P * PACK)
+JT = J // P
+TT = T // P
+CHUNK = 256
+CHUNKS = T // CHUNK
+BANK = 512
+
+
+def tile_list_page_of_hidden_values_pl_kernel(
+    tc, xt_words, xt_scales, wa_words, wa_scales, old, wb_words, wb_scales, offs, out_0, out_1, out_2
+):
+    nc = tc.nc
+    with ExitStack() as ctx:
+        sb = ctx.enter_context(tc.tile_pool(name="sb", bufs=1))
+        psum = ctx.enter_context(tc.psum_pool(name="psum", bufs=1))
+
+        def tile(shape, dtype, name, tag=None):
+            return sb.tile(shape, dtype, name=name, tag=tag or name, align_bytes=64)
+
+        def bank(b, name, dtype=F32, width=BANK):
+            return psum.tile([P, width], dtype, name=name, tag="bank%d" % b)
+
+        offsets = sb.tile([P, J // 16], U16, name="offsets")
+        x_words = [tile([P, T], U16, "x_words%d" % z) for z in range(PASSES)]
+        x_scales = tile([P, PASSES, T], U8, "x_scales")
+        a_words = tile([P, PASSES, R], U32, "a_words")
+        a_scales = tile([P, PASSES, R], U8, "a_scales")
+        b_scales = tile([P, N], U8, "b_scales")
+        page = [tile([P, T], F32, "page%d" % s) for s in range(PACK)]
+
+        nc.gpsimd.memset(x_scales[:].rearrange("p z c -> p (z c)").bitcast(U32), 0)
+        nc.vector.memset(a_scales[:].rearrange("p z c -> p (z c)").bitcast(U32), 0)
+        nc.vector.memset(b_scales[:].bitcast(U32), 0)
+
+        def load_scales(queue, plane, source):
+            for q in range(4):
+                queue.dma_start(
+                    out=plane[32 * q : 32 * q + 4].bitcast(I32),
+                    in_=source[:, 4 * q : 4 * q + 4, :].rearrange("z r c -> r z c").bitcast(I32),
+                )
+
+        old_dealt = old.rearrange("(p s) c -> s p c", s=PACK)
+        nc.sync.dma_start(offsets[:], offs)
+        nc.sync.dma_start(out=x_words[0][:].bitcast(I32), in_=xt_words[0].bitcast(I32))
+        load_scales(nc.scalar, x_scales, xt_scales)
+        nc.sync.dma_start(out=x_words[1][:].bitcast(I32), in_=xt_words[1].bitcast(I32))
+        nc.sync.dma_start(
+            out=a_words[:].bitcast(I32), in_=wa_words.rearrange("z p c r -> p z (c r)").bitcast(I32)
+        )
+        load_scales(nc.sync, a_scales, wa_scales)
+        load_scales(nc.sync, b_scales[:].rearrange("p (z c) -> p z c", z=1), wb_scales)
+
+        ident = tile([P, P], F32, "ident")
+        ident_bf = tile([P, P], BF16, "ident_bf")
+        make_identity(nc, ident[:])
+        make_identity(nc, ident_bf[:])
+        nc.vector.memset(page[0][:], 0.0)
+        nc.vector.memset(page[1][:], 0.0)
+        nc.gpsimd.memset(page[2][:], 0.0)
+        nc.gpsimd.memset(page[3][:], 0.0)
+
+        def entries(j0, j1):
+            return offsets[:, j0 // 16 : j1 // 16]
+
+        hidden = tile([P, PACK, J], F32, "hidden")
+        for jt in range(JT):
+            picked = entries(jt * P, (jt + 1) * P)
+            acc = bank(jt, "acc%d" % jt)
+            for z in range(PASSES):
+                g_words = tile([P, P], U16, "g_words%d_%d" % (jt, z))
+                g_scales = tile([P, P], U8, "g_scales%d_%d" % (jt, z))
+                nc.vector.tensor_copy(g_words[:], x_words[z][:].indirect(picked))
+                nc.vector.tensor_copy(g_scales[:], x_scales[:, z, :].indirect(picked))
+                nc.tensor.matmul_mx(
+                    out=acc[:],
+                    lhsT=g_words[:].bitcast(FP4X4),
+                    lhsT_scale=g_scales[:],
+                    rhs=a_words[:, z, :].bitcast(FP8X4),
+                    rhs_scale=a_scales[:, z, :],
+                    start=(z == 0),
+                    stop=(z == PASSES - 1),
+                )
+            a_sorted = tile([P, PACK, P], F32, "a_sorted%d" % jt)
+            nc.scalar.copy(out=a_sorted[:], in_=acc[:].rearrange("p (m s) -> p s m", s=PACK))
+            turned = bank(JT + jt, "turned%d" % jt)
+            for s in range(PACK):
+                nc.tensor.transpose(turned[:, s * P : (s + 1) * P], a_sorted[:, s, :], ident[:])
+            by_slot = turned[:].rearrange("p (s j) -> p s j", s=PACK)
+            cols = slice(jt * P, (jt + 1) * P)
+            nc.scalar.activation(out=hidden[:, 0:3, cols], in_=by_slot[:, 0:3, :], func=ACT.Relu, scale=2.0)
+            nc.scalar.activation(out=hidden[:, 3, cols], in_=by_slot[:, 3, :], func=ACT.Relu)
+
+        b_words = tile([P, N], U16, "b_words", "g_scales0_0")
+        nc.sync.dma_start(out=b_words[:].bitcast(I32), in_=wb_words[0].bitcast(I32))
+        old_rows = [tile([P, T], F32, "old_rows%d" % s, "g_words%d_%d" % divmod(s, PASSES)) for s in range(PACK)]
+        for s in range(PACK):
+            nc.sync.dma_start(out=old_rows[s][:], in_=old_dealt[s])
+
+        b_words_dealt = tile([P, PACK, P], U16, "b_words_dealt")
+        b_scales_dealt = tile([P, PACK, P], U8, "b_scales_dealt")
+        nc.vector.tensor_copy(b_words_dealt[:], b_words[:].rearrange("p (m s) -> p s m", s=PACK))
+        nc.vector.tensor_copy(b_scales_dealt[:], b_scales[:].rearrange("p (m s) -> p s m", s=PACK))
+
+        def scatter(s, j0, j1):
+            nc.vector.tensor_copy(page[s][:].indirect(entries(j0, j1)), hidden[:, s, j0:j1])
+
+        for j0, j1 in ((0, P), (P, 2 * P), (2 * P, J)):
+            scatter(0, j0, j1)
+            scatter(1, j0, j1)
+        scatter(2, 0, J)
+        scatter(3, 0, J)
+
+        def turn_into(sums, sources, terms, first):
+            for i, (s, k) in enumerate(terms):
+                nc.tensor.matmul(
+                    sums[:, i * P : (i + 1) * P], sources[s][:, k * P : (k + 1) * P], ident[:],
+                    start=(first and i == 0), stop=(not first and i == len(terms) - 1), is_transpose=True,
+                )
+
+        grouped = [tile([P, CHUNK, PACK], BF16, "grouped%d" % c) for c in range(CHUNKS)]
+        upper = [tile([P, 2, CHUNK], BF16, "upper%d" % c) for c in range(CHUNKS)]
+
+        pair_terms = [[(s, 2 * c + kk) for kk in range(2) for s in range(2)] for c in range(CHUNKS)]
+        pair_sums = [bank(c, "pair_sums%d" % c) for c in range(CHUNKS)]
+        back = [bank(6 + h, "back%d" % h) for h in range(2)]
+        for c in range(CHUNKS):
+            turn_into(pair_sums[c], old_rows, pair_terms[c], True)
+        for c in range(CHUNKS):
+            turn_into(pair_sums[c], page, pair_terms[c], False)
+        for c in range(CHUNKS):
+            pairs = tile([P, 2, P, 2], BF16, "pairs%d" % c)
+            nc.scalar.activation(
+                out=pairs[:], in_=pair_sums[c][:].rearrange("p (k s m) -> p k m s", k=2, s=2),
+                func=ACT.Copy, scale=0.5,
+            )
+            pair_words = pairs[:].rearrange("p k m s -> p (k m s)").bitcast(F32)
+            for kk in range(2):
+                k = 2 * (c % 2) + kk
+                nc.tensor.transpose(back[c // 2][:, k * P : (k + 1) * P], pair_words[:, kk * P : (kk + 1) * P], ident[:])
+
+        def place_pairs(c):
+            words = grouped[c][:].rearrange("p c s -> p (c s)").bitcast(F32).rearrange("p (c u) -> p c u", u=2)
+            nc.scalar.copy(out=words[:, :, 0], in_=back[c // 2][:, (c % 2) * CHUNK : (c % 2 + 1) * CHUNK])
+
+        def third_slot(h):
+            sums = bank(2 + h, "third_sums%d" % h)
+            terms = [(2, 4 * h + kk) for kk in range(4)]
+            turn_into(sums, old_rows, terms, True)
+            turn_into(sums, page, terms, False)
+            third = tile([P, BANK], BF16, "third%d" % h)
+            nc.scalar.activation(out=third[:], in_=sums[:], func=ACT.Copy, scale=0.5)
+            third_back = bank(h, "third_back%d" % h, BF16)
+            for kk in range(4):
+                nc.tensor.transpose(third_back[:, kk * P : (kk + 1) * P], third[:, kk * P : (kk + 1) * P], ident_bf[:])
+            for i in range(2):
+                nc.scalar.copy(out=upper[2 * h + i][:, 0, :], in_=third_back[:, i * CHUNK : (i + 1) * CHUNK])
+
+        place_pairs(0)
+        place_pairs(1)
+        third_slot(0)
+        place_pairs(2)
+        third_slot(1)
+        place_pairs(3)
+
+        y_words = tile([P, T], U32, "y_words")
+        y_scales = tile([P, T], U8, "y_scales")
+        out_dealt = out_0.rearrange("(p s) c -> p s c", s=PACK)
+        out_words = out_1[0].rearrange("p c r -> p (c r)").bitcast(I32)
+        y_banks = ((4, 5), (6, 2), (0, 7), (3, 1))
+
+        p_words = [tile([P, CHUNK], U32, "p_words%d" % c) for c in range(CHUNKS)]
+        p_scales = [tile([P, CHUNK], U8, "p_scales%d" % c) for c in range(CHUNKS)]
+        y = [tile([P, PACK, CHUNK], F32, "y%d" % c) for c in range(CHUNKS)]
+        y_grouped = [tile([P, CHUNK, PACK], BF16, "y_grouped%d" % c) for c in range(CHUNKS)]
+
+        def span(c):
+            return slice(c * CHUNK, (c + 1) * CHUNK)
+
+        def add_last(c):
+            nc.vector.scalar_tensor_tensor(
+                out=upper[c][:, 1, :], in0=old_rows[3][:, span(c)], scalar=0.5, in1=page[3][:, span(c)],
+                op0=ALU.mult, op1=ALU.add,
+            )
+
+        def weave(c):
+            dst = grouped[c][:, :, 2:4]
+            src = upper[c][:].rearrange("p s c -> p c s")
+            if c == 1:
+                nc.scalar.copy(out=dst, in_=src)
+            else:
+                nc.vector.tensor_copy(out=dst, in_=src)
+
+        def quantise_page(c):
+            nc.vector.quantize_mx(
+                out=p_words[c][:].bitcast(FP8X4), scales=p_scales[c][:],
+                in_=grouped[c][:].rearrange("p c s -> p (c s)"),
+            )
+
+        def second_layer(c):
+            for h in range(2):
+                acc = bank(y_banks[c][h], "y_acc%d_%d" % (c, h))
+                for i in range(2):
+                    s = 2 * h + i
+                    nc.tensor.matmul_mx(
+                        out=acc[:, i * CHUNK : (i + 1) * CHUNK],
+                        lhsT=b_words_dealt[:, s, :].bitcast(FP4X4),
+                        lhsT_scale=b_scales_dealt[:, s, :],
+                        rhs=p_words[c][:].bitcast(FP8X4),
+                        rhs_scale=p_scales[c][:],
+                        start=True,
+                        stop=True,
+                    )
+                nc.scalar.copy(out=y[c][:, 2 * h : 2 * h + 2, :], in_=acc[:].rearrange("p (i c) -> p i c", i=2))
+            nc.sync.dma_start(out=out_dealt[:, :, span(c)], in_=y[c][:])
+
+        def round_y(c):
+            nc.vector.tensor_copy(
+                out=y_grouped[c][:].rearrange("p (c i) s -> p c s i", i=4),
+                in_=y[c][:].rearrange("p s (c i) -> p c s i", i=4),
+            )
+
+        def quantise_y(c):
+            nc.vector.quantize_mx(
+                out=y_words[:, span(c)].bitcast(FP8X4), scales=y_scales[:, span(c)],
+                in_=y_grouped[c][:].rearrange("p c s -> p (c s)"),
+            )
+            nc.sync.dma_start(out=out_words[:, span(c)], in_=y_words[:, span(c)].bitcast(I32))
+
+        add_last(0)
+        add_last(1)
+        weave(0)
+        weave(1)
+        add_last(2)
+        quantise_page(0)
+        second_layer(0)
+        add_last(3)
+        quantise_page(1)
+        second_layer(1)
+        weave(2)
+        weave(3)
+        quantise_page(2)
+        second_layer(2)
+        round_y(0)
+        quantise_page(3)
+        second_layer(3)
+        quantise_y(0)
+        for c in range(1, CHUNKS):
+            round_y(c)
+            quantise_y(c)
+        for q in range(4):
+            queue = nc.sync if q % 2 == 0 else nc.scalar
+            queue.dma_start(
+                out=out_2[0, 4 * q : 4 * q + 4, :].bitcast(I32), in_=y_scales[32 * q : 32 * q + 4, :].bitcast(I32)
+            )

@@ -47,55 +47,54 @@ def tile_list_page_of_hidden_values_pl_kernel(
         a_words = tile([P, PASSES, R], U32, "a_words")
         a_scales = tile([P, PASSES, R], U8, "a_scales")
         b_scales = tile([P, N], U8, "b_scales")
-        page = [tile([P, T], F32, "page%d" % s) for s in range(PACK)]
+        page = [tile([P, T], F32, "page%d" % s) for s in range(3)]
 
         nc.gpsimd.memset(x_scales[:].rearrange("p z c -> p (z c)").bitcast(U32), 0)
         nc.vector.memset(a_scales[:].rearrange("p z c -> p (z c)").bitcast(U32), 0)
         nc.vector.memset(b_scales[:].bitcast(U32), 0)
 
-        def load_scales(queue, plane, source):
+        def load_scales(plane, source):
             for q in range(4):
-                queue.dma_start(
+                nc.sync.dma_start(
                     out=plane[32 * q : 32 * q + 4].bitcast(I32),
                     in_=source[:, 4 * q : 4 * q + 4, :].rearrange("z r c -> r z c").bitcast(I32),
                 )
 
         old_dealt = old.rearrange("(p s) c -> s p c", s=PACK)
+        for z in range(PASSES):
+            nc.sync.dma_start(out=x_words[z][:].bitcast(I32), in_=xt_words[z].bitcast(I32))
+        load_scales(x_scales, xt_scales)
         nc.sync.dma_start(offsets[:], offs)
-        nc.sync.dma_start(out=x_words[0][:].bitcast(I32), in_=xt_words[0].bitcast(I32))
-        load_scales(nc.scalar, x_scales, xt_scales)
-        nc.sync.dma_start(out=x_words[1][:].bitcast(I32), in_=xt_words[1].bitcast(I32))
         nc.sync.dma_start(
             out=a_words[:].bitcast(I32), in_=wa_words.rearrange("z p c r -> p z (c r)").bitcast(I32)
         )
-        load_scales(nc.sync, a_scales, wa_scales)
-        load_scales(nc.sync, b_scales[:].rearrange("p (z c) -> p z c", z=1), wb_scales)
+        load_scales(a_scales, wa_scales)
+        load_scales(b_scales[:].rearrange("p (z c) -> p z c", z=1), wb_scales)
 
         ident = tile([P, P], F32, "ident")
-        ident_bf = tile([P, P], BF16, "ident_bf")
         make_identity(nc, ident[:])
-        make_identity(nc, ident_bf[:])
         nc.vector.memset(page[0][:], 0.0)
         nc.vector.memset(page[1][:], 0.0)
         nc.gpsimd.memset(page[2][:], 0.0)
-        nc.gpsimd.memset(page[3][:], 0.0)
 
         def entries(j0, j1):
             return offsets[:, j0 // 16 : j1 // 16]
 
         hidden = tile([P, PACK, J], F32, "hidden")
+        g_scales = {}
         for jt in range(JT):
             picked = entries(jt * P, (jt + 1) * P)
-            acc = bank(jt, "acc%d" % jt)
+            acc = bank(jt % 2, "acc%d" % jt)
             for z in range(PASSES):
                 g_words = tile([P, P], U16, "g_words%d_%d" % (jt, z))
-                g_scales = tile([P, P], U8, "g_scales%d_%d" % (jt, z))
+                if jt % 2 == 0:
+                    g_scales[z] = tile([P, 2 * P], U8, "g_scales%d_%d" % (jt, z))
+                    nc.vector.tensor_copy(g_scales[z][:], x_scales[:, z, :].indirect(entries(jt * P, (jt + 2) * P)))
                 nc.vector.tensor_copy(g_words[:], x_words[z][:].indirect(picked))
-                nc.vector.tensor_copy(g_scales[:], x_scales[:, z, :].indirect(picked))
                 nc.tensor.matmul_mx(
                     out=acc[:],
                     lhsT=g_words[:].bitcast(FP4X4),
-                    lhsT_scale=g_scales[:],
+                    lhsT_scale=g_scales[z][:, (jt % 2) * P : (jt % 2 + 1) * P],
                     rhs=a_words[:, z, :].bitcast(FP8X4),
                     rhs_scale=a_scales[:, z, :],
                     start=(z == 0),
@@ -108,12 +107,12 @@ def tile_list_page_of_hidden_values_pl_kernel(
                 nc.tensor.transpose(turned[:, s * P : (s + 1) * P], a_sorted[:, s, :], ident[:])
             by_slot = turned[:].rearrange("p (s j) -> p s j", s=PACK)
             cols = slice(jt * P, (jt + 1) * P)
-            nc.scalar.activation(out=hidden[:, 0:3, cols], in_=by_slot[:, 0:3, :], func=ACT.Relu, scale=2.0)
-            nc.scalar.activation(out=hidden[:, 3, cols], in_=by_slot[:, 3, :], func=ACT.Relu)
+            nc.scalar.activation(out=hidden[:, 0:2, cols], in_=by_slot[:, 0:2, :], func=ACT.Relu, scale=2.0)
+            nc.scalar.activation(out=hidden[:, 2:4, cols], in_=by_slot[:, 2:4, :], func=ACT.Relu)
 
-        b_words = tile([P, N], U16, "b_words", "g_scales0_0")
+        b_words = tile([P, N], U16, "b_words", "g_words0_0")
         nc.sync.dma_start(out=b_words[:].bitcast(I32), in_=wb_words[0].bitcast(I32))
-        old_rows = [tile([P, T], F32, "old_rows%d" % s, "g_words%d_%d" % divmod(s, PASSES)) for s in range(PACK)]
+        old_rows = [tile([P, T], F32, "old_rows%d" % s, "g_words%d_%d" % divmod(s + 1, PASSES)) for s in range(PACK)]
         for s in range(PACK):
             nc.sync.dma_start(out=old_rows[s][:], in_=old_dealt[s])
 
@@ -123,13 +122,11 @@ def tile_list_page_of_hidden_values_pl_kernel(
         nc.vector.tensor_copy(b_scales_dealt[:], b_scales[:].rearrange("p (m s) -> p s m", s=PACK))
 
         def scatter(s, j0, j1):
-            nc.vector.tensor_copy(page[s][:].indirect(entries(j0, j1)), hidden[:, s, j0:j1])
+            nc.vector.tensor_copy(page[s % 3][:].indirect(entries(j0, j1)), hidden[:, s, j0:j1])
 
-        for j0, j1 in ((0, P), (P, 2 * P), (2 * P, J)):
-            scatter(0, j0, j1)
-            scatter(1, j0, j1)
-        scatter(2, 0, J)
-        scatter(3, 0, J)
+        for jt in range(JT):
+            scatter(0, jt * P, (jt + 1) * P)
+            scatter(1, jt * P, (jt + 1) * P)
 
         def turn_into(sums, sources, terms, first):
             for i, (s, k) in enumerate(terms):
@@ -139,7 +136,6 @@ def tile_list_page_of_hidden_values_pl_kernel(
                 )
 
         grouped = [tile([P, CHUNK, PACK], BF16, "grouped%d" % c) for c in range(CHUNKS)]
-        upper = [tile([P, 2, CHUNK], BF16, "upper%d" % c) for c in range(CHUNKS)]
 
         pair_terms = [[(s, 2 * c + kk) for kk in range(2) for s in range(2)] for c in range(CHUNKS)]
         pair_sums = [bank(c, "pair_sums%d" % c) for c in range(CHUNKS)]
@@ -148,6 +144,8 @@ def tile_list_page_of_hidden_values_pl_kernel(
             turn_into(pair_sums[c], old_rows, pair_terms[c], True)
         for c in range(CHUNKS):
             turn_into(pair_sums[c], page, pair_terms[c], False)
+        scatter(2, 0, J)
+        scatter(3, 0, J)
         for c in range(CHUNKS):
             pairs = tile([P, 2, P, 2], BF16, "pairs%d" % c)
             nc.scalar.activation(
@@ -163,31 +161,14 @@ def tile_list_page_of_hidden_values_pl_kernel(
             words = grouped[c][:].rearrange("p c s -> p (c s)").bitcast(F32).rearrange("p (c u) -> p c u", u=2)
             nc.scalar.copy(out=words[:, :, 0], in_=back[c // 2][:, (c % 2) * CHUNK : (c % 2 + 1) * CHUNK])
 
-        def third_slot(h):
-            sums = bank(2 + h, "third_sums%d" % h)
-            terms = [(2, 4 * h + kk) for kk in range(4)]
-            turn_into(sums, old_rows, terms, True)
-            turn_into(sums, page, terms, False)
-            third = tile([P, BANK], BF16, "third%d" % h)
-            nc.scalar.activation(out=third[:], in_=sums[:], func=ACT.Copy, scale=0.5)
-            third_back = bank(h, "third_back%d" % h, BF16)
-            for kk in range(4):
-                nc.tensor.transpose(third_back[:, kk * P : (kk + 1) * P], third[:, kk * P : (kk + 1) * P], ident_bf[:])
-            for i in range(2):
-                nc.scalar.copy(out=upper[2 * h + i][:, 0, :], in_=third_back[:, i * CHUNK : (i + 1) * CHUNK])
-
-        place_pairs(0)
-        place_pairs(1)
-        third_slot(0)
-        place_pairs(2)
-        third_slot(1)
-        place_pairs(3)
+        for c in range(CHUNKS):
+            place_pairs(c)
 
         y_words = tile([P, T], U32, "y_words")
         y_scales = tile([P, T], U8, "y_scales")
         out_dealt = out_0.rearrange("(p s) c -> p s c", s=PACK)
         out_words = out_1[0].rearrange("p c r -> p (c r)").bitcast(I32)
-        y_banks = ((4, 5), (6, 2), (0, 7), (3, 1))
+        y_banks = ((4, 5), (0, 1), (2, 3), (6, 7))
 
         p_words = [tile([P, CHUNK], U32, "p_words%d" % c) for c in range(CHUNKS)]
         p_scales = [tile([P, CHUNK], U8, "p_scales%d" % c) for c in range(CHUNKS)]
@@ -197,16 +178,20 @@ def tile_list_page_of_hidden_values_pl_kernel(
         def span(c):
             return slice(c * CHUNK, (c + 1) * CHUNK)
 
-        def add_last(c):
-            nc.vector.scalar_tensor_tensor(
-                out=upper[c][:, 1, :], in0=old_rows[3][:, span(c)], scalar=0.5, in1=page[3][:, span(c)],
-                op0=ALU.mult, op1=ALU.add,
-            )
+        upper = {}
+
+        def add_upper(c):
+            upper[c] = tile([P, 2, CHUNK], BF16, "upper%d" % c, "upper%d" % (c % 2))
+            for s in (2, 3):
+                nc.vector.scalar_tensor_tensor(
+                    out=upper[c][:, s - 2, :], in0=old_rows[s][:, span(c)], scalar=0.5, in1=page[s % 3][:, span(c)],
+                    op0=ALU.mult, op1=ALU.add,
+                )
 
         def weave(c):
             dst = grouped[c][:, :, 2:4]
             src = upper[c][:].rearrange("p s c -> p c s")
-            if c == 1:
+            if c in (1, 2):
                 nc.scalar.copy(out=dst, in_=src)
             else:
                 nc.vector.tensor_copy(out=dst, in_=src)
@@ -234,6 +219,27 @@ def tile_list_page_of_hidden_values_pl_kernel(
                 nc.scalar.copy(out=y[c][:, 2 * h : 2 * h + 2, :], in_=acc[:].rearrange("p (i c) -> p i c", i=2))
             nc.sync.dma_start(out=out_dealt[:, :, span(c)], in_=y[c][:])
 
+        def second_layer_last(c):
+            half = CHUNK // 2
+            accs = [bank(y_banks[c][h], "y_acc%d_%d" % (c, h)) for h in range(2)]
+            for h in range(2):
+                cols = slice(h * half, (h + 1) * half)
+                for s in range(PACK):
+                    nc.tensor.matmul_mx(
+                        out=accs[h][:, s * half : (s + 1) * half],
+                        lhsT=b_words_dealt[:, s, :].bitcast(FP4X4),
+                        lhsT_scale=b_scales_dealt[:, s, :],
+                        rhs=p_words[c][:, cols].bitcast(FP8X4),
+                        rhs_scale=p_scales[c][:, cols],
+                        start=True,
+                        stop=True,
+                    )
+                nc.scalar.copy(out=y_grouped[c][:, cols, :], in_=accs[h][:].rearrange("p (s c) -> p c s", s=PACK))
+            for h in range(2):
+                cols = slice(h * half, (h + 1) * half)
+                nc.scalar.copy(out=y[c][:, :, cols], in_=accs[h][:].rearrange("p (s c) -> p s c", s=PACK))
+            nc.sync.dma_start(out=out_dealt[:, :, span(c)], in_=y[c][:])
+
         def round_y(c):
             nc.vector.tensor_copy(
                 out=y_grouped[c][:].rearrange("p (c i) s -> p c s i", i=4),
@@ -247,26 +253,27 @@ def tile_list_page_of_hidden_values_pl_kernel(
             )
             nc.sync.dma_start(out=out_words[:, span(c)], in_=y_words[:, span(c)].bitcast(I32))
 
-        add_last(0)
-        add_last(1)
+        add_upper(0)
         weave(0)
+        add_upper(1)
         weave(1)
-        add_last(2)
         quantise_page(0)
         second_layer(0)
-        add_last(3)
+        add_upper(2)
+        weave(2)
         quantise_page(1)
         second_layer(1)
-        weave(2)
+        add_upper(3)
         weave(3)
         quantise_page(2)
         second_layer(2)
-        round_y(0)
         quantise_page(3)
-        second_layer(3)
+        second_layer_last(3)
+        round_y(0)
         quantise_y(0)
         for c in range(1, CHUNKS):
-            round_y(c)
+            if c < CHUNKS - 1:
+                round_y(c)
             quantise_y(c)
         for q in range(4):
             queue = nc.sync if q % 2 == 0 else nc.scalar

@@ -108,7 +108,7 @@ def tile_list_page_of_hidden_values_pl_kernel(
             by_slot = turned[:].rearrange("p (s j) -> p s j", s=PACK)
             cols = slice(jt * P, (jt + 1) * P)
             nc.scalar.activation(out=hidden[:, 0:2, cols], in_=by_slot[:, 0:2, :], func=ACT.Relu, scale=2.0)
-            nc.scalar.activation(out=hidden[:, 2:4, cols], in_=by_slot[:, 2:4, :], func=ACT.Relu)
+            nc.scalar.activation(out=hidden[:, 2:4, cols], in_=by_slot[:, 2:4, :], func=ACT.Relu, scale=2.0)
 
         b_words = tile([P, N], U16, "b_words", "g_words0_0")
         nc.sync.dma_start(out=b_words[:].bitcast(I32), in_=wb_words[0].bitcast(I32))
@@ -178,23 +178,22 @@ def tile_list_page_of_hidden_values_pl_kernel(
         def span(c):
             return slice(c * CHUNK, (c + 1) * CHUNK)
 
-        upper = {}
+        upper = tile([P, CHUNKS + 2, CHUNK], BF16, "upper")
+        nc.gpsimd.tensor_tensor(
+            upper[:, 0:CHUNKS, :].rearrange("p k c -> p (k c)"), page[2][:], old_rows[2][:], ALU.add
+        )
 
         def add_upper(c):
-            upper[c] = tile([P, 2, CHUNK], BF16, "upper%d" % c, "upper%d" % (c % 2))
-            for s in (2, 3):
-                nc.vector.scalar_tensor_tensor(
-                    out=upper[c][:, s - 2, :], in0=old_rows[s][:, span(c)], scalar=0.5, in1=page[s % 3][:, span(c)],
-                    op0=ALU.mult, op1=ALU.add,
-                )
+            nc.vector.tensor_tensor(upper[:, CHUNKS + c % 2, :], page[0][:, span(c)], old_rows[3][:, span(c)], ALU.add)
 
         def weave(c):
             dst = grouped[c][:, :, 2:4]
-            src = upper[c][:].rearrange("p s c -> p c s")
-            if c in (1, 2):
-                nc.scalar.copy(out=dst, in_=src)
+            last = CHUNKS + c % 2
+            src = upper[:, c : last + 1 : last - c, :].rearrange("p s c -> p c s")
+            if c == 1:
+                nc.scalar.activation(out=dst, in_=src, func=ACT.Copy, scale=0.5)
             else:
-                nc.vector.tensor_copy(out=dst, in_=src)
+                nc.vector.tensor_scalar_mul(dst, src, 0.5)
 
         def quantise_page(c):
             nc.vector.quantize_mx(
@@ -254,8 +253,8 @@ def tile_list_page_of_hidden_values_pl_kernel(
             nc.sync.dma_start(out=out_words[:, span(c)], in_=y_words[:, span(c)].bitcast(I32))
 
         add_upper(0)
-        weave(0)
         add_upper(1)
+        weave(0)
         weave(1)
         quantise_page(0)
         second_layer(0)

from contextlib import ExitStack

import concourse.mybir as mybir
from concourse.masks import make_identity

K, T, J, R, N = 1024, 1024, 512, 512, 512
FLOPS = 2 * K * R * J + 2 * R * N * T

F32 = mybir.dt.float32
BF16 = mybir.dt.bfloat16
I32 = mybir.dt.int32
U32 = mybir.dt.uint32
U16 = mybir.dt.uint16
U8 = mybir.dt.uint8
FP8X4 = mybir.dt.float8_e4m3fn_x4
FP4X4 = mybir.dt.float4_e2m1fn_x4
ACT = mybir.ActivationFunctionType
ALU = mybir.AluOpType

P = 128
PACK = 4
PASSES = K // (P * PACK)
JT = J // P
TT = T // P
CHUNK = 256
CHUNKS = T // CHUNK
BANK = 512


def tile_list_page_of_hidden_values_pl_kernel(
    tc, xt_words, xt_scales, wa_words, wa_scales, old, wb_words, wb_scales, offs, out_0, out_1, out_2
):
    nc = tc.nc
    with ExitStack() as ctx:
        sb = ctx.enter_context(tc.tile_pool(name="sb", bufs=1))
        psum = ctx.enter_context(tc.psum_pool(name="psum", bufs=1))

        def tile(shape, dtype, name, tag=None):
            return sb.tile(shape, dtype, name=name, tag=tag or name, align_bytes=64)

        def bank(b, name, dtype=F32, width=BANK):
            return psum.tile([P, width], dtype, name=name, tag="bank%d" % b)

        offsets = sb.tile([P, J // 16], U16, name="offsets")
        x_words = [tile([P, T], U16, "x_words%d" % z) for z in range(PASSES)]
        x_scales = tile([P, PASSES, T], U8, "x_scales")
        a_words = tile([P, PASSES, R], U32, "a_words")
        a_scales = tile([P, PASSES, R], U8, "a_scales")
        b_scales = tile([P, N], U8, "b_scales")
        page = [tile([P, T], F32, "page%d" % s) for s in range(3)]

        nc.gpsimd.memset(x_scales[:].rearrange("p z c -> p (z c)").bitcast(U32), 0)
        nc.vector.memset(a_scales[:].rearrange("p z c -> p (z c)").bitcast(U32), 0)
        nc.vector.memset(b_scales[:].bitcast(U32), 0)

        def load_scales(plane, source):
            for q in range(4):
                nc.sync.dma_start(
                    out=plane[32 * q : 32 * q + 4].bitcast(I32),
                    in_=source[:, 4 * q : 4 * q + 4, :].rearrange("z r c -> r z c").bitcast(I32),
                )

        old_dealt = old.rearrange("(p s) c -> s p c", s=PACK)
        for z in range(PASSES):
            nc.sync.dma_start(out=x_words[z][:].bitcast(I32), in_=xt_words[z].bitcast(I32))
        load_scales(x_scales, xt_scales)
        nc.sync.dma_start(offsets[:], offs)
        nc.sync.dma_start(
            out=a_words[:].bitcast(I32), in_=wa_words.rearrange("z p c r -> p z (c r)").bitcast(I32)
        )
        load_scales(a_scales, wa_scales)
        load_scales(b_scales[:].rearrange("p (z c) -> p z c", z=1), wb_scales)

        ident = tile([P, P], F32, "ident")
        make_identity(nc, ident[:])
        nc.vector.memset(page[0][:], 0.0)
        nc.vector.memset(page[1][:], 0.0)
        nc.gpsimd.memset(page[2][:], 0.0)

        def entries(j0, j1):
            return offsets[:, j0 // 16 : j1 // 16]

        hidden = tile([P, PACK, J], F32, "hidden")
        g_scales = {}
        for jt in range(JT):
            picked = entries(jt * P, (jt + 1) * P)
            acc = bank(jt % 2, "acc%d" % jt)
            for z in range(PASSES):
                g_words = tile([P, P], U16, "g_words%d_%d" % (jt, z))
                if jt % 2 == 0:
                    g_scales[z] = tile([P, 2 * P], U8, "g_scales%d_%d" % (jt, z))
                    nc.vector.tensor_copy(g_scales[z][:], x_scales[:, z, :].indirect(entries(jt * P, (jt + 2) * P)))
                nc.vector.tensor_copy(g_words[:], x_words[z][:].indirect(picked))
                nc.tensor.matmul_mx(
                    out=acc[:],
                    lhsT=g_words[:].bitcast(FP4X4),
                    lhsT_scale=g_scales[z][:, (jt % 2) * P : (jt % 2 + 1) * P],
                    rhs=a_words[:, z, :].bitcast(FP8X4),
                    rhs_scale=a_scales[:, z, :],
                    start=(z == 0),
                    stop=(z == PASSES - 1),
                )
            a_sorted = tile([P, PACK, P], F32, "a_sorted%d" % jt)
            nc.scalar.copy(out=a_sorted[:], in_=acc[:].rearrange("p (m s) -> p s m", s=PACK))
            turned = bank(JT + jt, "turned%d" % jt)
            for s in range(PACK):
                nc.tensor.transpose(turned[:, s * P : (s + 1) * P], a_sorted[:, s, :], ident[:])
            by_slot = turned[:].rearrange("p (s j) -> p s j", s=PACK)
            cols = slice(jt * P, (jt + 1) * P)
            nc.scalar.activation(out=hidden[:, 0:2, cols], in_=by_slot[:, 0:2, :], func=ACT.Relu, scale=2.0)
            nc.scalar.activation(out=hidden[:, 2:4, cols], in_=by_slot[:, 2:4, :], func=ACT.Relu, scale=2.0)

        b_words = tile([P, N], U16, "b_words", "g_words0_0")
        nc.sync.dma_start(out=b_words[:].bitcast(I32), in_=wb_words[0].bitcast(I32))
        old_rows = [tile([P, T], F32, "old_rows%d" % s, "g_words%d_%d" % divmod(s + 1, PASSES)) for s in range(PACK)]
        for s in range(PACK):
            nc.sync.dma_start(out=old_rows[s][:], in_=old_dealt[s])

        b_words_dealt = tile([P, PACK, P], U16, "b_words_dealt")
        b_scales_dealt = tile([P, PACK, P], U8, "b_scales_dealt")
        nc.vector.tensor_copy(b_words_dealt[:], b_words[:].rearrange("p (m s) -> p s m", s=PACK))
        nc.vector.tensor_copy(b_scales_dealt[:], b_scales[:].rearrange("p (m s) -> p s m", s=PACK))

        def scatter(s, j0, j1):
            nc.vector.tensor_copy(page[s % 3][:].indirect(entries(j0, j1)), hidden[:, s, j0:j1])

        for jt in range(JT):
            scatter(0, jt * P, (jt + 1) * P)
            scatter(1, jt * P, (jt + 1) * P)

        def turn_into(sums, sources, terms, first):
            for i, (s, k) in enumerate(terms):
                nc.tensor.matmul(
                    sums[:, i * P : (i + 1) * P], sources[s][:, k * P : (k + 1) * P], ident[:],
                    start=(first and i == 0), stop=(not first and i == len(terms) - 1), is_transpose=True,
                )

        grouped = [tile([P, CHUNK, PACK], BF16, "grouped%d" % c) for c in range(CHUNKS)]

        pair_terms = [[(s, 2 * c + kk) for kk in range(2) for s in range(2)] for c in range(CHUNKS)]
        pair_sums = [bank(c, "pair_sums%d" % c) for c in range(CHUNKS)]
        back = [bank(6 + h, "back%d" % h) for h in range(2)]
        for c in range(CHUNKS):
            turn_into(pair_sums[c], old_rows, pair_terms[c], True)
        for c in range(CHUNKS):
            turn_into(pair_sums[c], page, pair_terms[c], False)
        scatter(2, 0, J)
        scatter(3, 0, J)
        for c in range(CHUNKS):
            pairs = tile([P, 2, P, 2], BF16, "pairs%d" % c)
            nc.scalar.activation(
                out=pairs[:], in_=pair_sums[c][:].rearrange("p (k s m) -> p k m s", k=2, s=2),
                func=ACT.Copy, scale=0.5,
            )
            pair_words = pairs[:].rearrange("p k m s -> p (k m s)").bitcast(F32)
            for kk in range(2):
                k = 2 * (c % 2) + kk
                nc.tensor.transpose(back[c // 2][:, k * P : (k + 1) * P], pair_words[:, kk * P : (kk + 1) * P], ident[:])

        def place_pairs(c):
            words = grouped[c][:].rearrange("p c s -> p (c s)").bitcast(F32).rearrange("p (c u) -> p c u", u=2)
            nc.scalar.copy(out=words[:, :, 0], in_=back[c // 2][:, (c % 2) * CHUNK : (c % 2 + 1) * CHUNK])

        for c in range(CHUNKS):
            place_pairs(c)

        y_words = tile([P, T], U32, "y_words")
        y_scales = tile([P, T], U8, "y_scales")
        out_dealt = out_0.rearrange("(p s) c -> p s c", s=PACK)
        out_words = out_1[0].rearrange("p c r -> p (c r)").bitcast(I32)
        y_banks = ((4, 5), (0, 1), (2, 3), (6, 7))

        p_words = [tile([P, CHUNK], U32, "p_words%d" % c) for c in range(CHUNKS)]
        p_scales = [tile([P, CHUNK], U8, "p_scales%d" % c) for c in range(CHUNKS)]
        y = [tile([P, PACK, CHUNK], F32, "y%d" % c) for c in range(CHUNKS)]
        y_grouped = [tile([P, CHUNK, PACK], BF16, "y_grouped%d" % c) for c in range(CHUNKS)]

        def span(c):
            return slice(c * CHUNK, (c + 1) * CHUNK)

        upper = tile([P, CHUNKS + 2, CHUNK], BF16, "upper")
        nc.gpsimd.tensor_tensor(
            upper[:, 0:CHUNKS, :].rearrange("p k c -> p (k c)"), page[2][:], old_rows[2][:], ALU.add
        )

        def add_upper(c):
            nc.vector.tensor_tensor(upper[:, CHUNKS + c % 2, :], page[0][:, span(c)], old_rows[3][:, span(c)], ALU.add)

        def weave(c):
            dst = grouped[c][:, :, 2:4]
            last = CHUNKS + c % 2
            src = upper[:, c : last + 1 : last - c, :].rearrange("p s c -> p c s")
            if c == 1:
                nc.scalar.activation(out=dst, in_=src, func=ACT.Copy, scale=0.5)
            else:
                nc.vector.tensor_scalar_mul(dst, src, 0.5)

        def quantise_page(c):
            nc.vector.quantize_mx(
                out=p_words[c][:].bitcast(FP8X4), scales=p_scales[c][:],
                in_=grouped[c][:].rearrange("p c s -> p (c s)"),
            )

        def second_layer(c):
            for h in range(2):
                acc = bank(y_banks[c][h], "y_acc%d_%d" % (c, h))
                for i in range(2):
                    s = 2 * h + i
                    nc.tensor.matmul_mx(
                        out=acc[:, i * CHUNK : (i + 1) * CHUNK],
                        lhsT=b_words_dealt[:, s, :].bitcast(FP4X4),
                        lhsT_scale=b_scales_dealt[:, s, :],
                        rhs=p_words[c][:].bitcast(FP8X4),
                        rhs_scale=p_scales[c][:],
                        start=True,
                        stop=True,
                    )
                nc.scalar.copy(out=y[c][:, 2 * h : 2 * h + 2, :], in_=acc[:].rearrange("p (i c) -> p i c", i=2))
            nc.sync.dma_start(out=out_dealt[:, :, span(c)], in_=y[c][:])

        def second_layer_last(c):
            half = CHUNK // 2
            accs = [bank(y_banks[c][h], "y_acc%d_%d" % (c, h)) for h in range(2)]
            for h in range(2):
                cols = slice(h * half, (h + 1) * half)
                for s in range(PACK):
                    nc.tensor.matmul_mx(
                        out=accs[h][:, s * half : (s + 1) * half],
                        lhsT=b_words_dealt[:, s, :].bitcast(FP4X4),
                        lhsT_scale=b_scales_dealt[:, s, :],
                        rhs=p_words[c][:, cols].bitcast(FP8X4),
                        rhs_scale=p_scales[c][:, cols],
                        start=True,
                        stop=True,
                    )
                nc.scalar.copy(out=y_grouped[c][:, cols, :], in_=accs[h][:].rearrange("p (s c) -> p c s", s=PACK))
            for h in range(2):
                cols = slice(h * half, (h + 1) * half)
                nc.scalar.copy(out=y[c][:, :, cols], in_=accs[h][:].rearrange("p (s c) -> p s c", s=PACK))
            nc.sync.dma_start(out=out_dealt[:, :, span(c)], in_=y[c][:])

        def round_y(c):
            nc.vector.tensor_copy(
                out=y_grouped[c][:].rearrange("p (c i) s -> p c s i", i=4),
                in_=y[c][:].rearrange("p s (c i) -> p c s i", i=4),
            )

        def quantise_y(c):
            nc.vector.quantize_mx(
                out=y_words[:, span(c)].bitcast(FP8X4), scales=y_scales[:, span(c)],
                in_=y_grouped[c][:].rearrange("p c s -> p (c s)"),
            )
            nc.sync.dma_start(out=out_words[:, span(c)], in_=y_words[:, span(c)].bitcast(I32))

        add_upper(0)
        add_upper(1)
        weave(0)
        weave(1)
        quantise_page(0)
        second_layer(0)
        add_upper(2)
        weave(2)
        quantise_page(1)
        second_layer(1)
        add_upper(3)
        weave(3)
        quantise_page(2)
        second_layer(2)
        quantise_page(3)
        second_layer_last(3)
        round_y(0)
        quantise_y(0)
        for c in range(1, CHUNKS):
            if c < CHUNKS - 1:
                round_y(c)
            quantise_y(c)
        for q in range(4):
            queue = nc.sync if q % 2 == 0 else nc.scalar
            queue.dma_start(
                out=out_2[0, 4 * q : 4 * q + 4, :].bitcast(I32), in_=y_scales[32 * q : 32 * q + 4, :].bitcast(I32)
            )
